import numpy as np
import ml_dtypes


def mxq(x, axis, fmt="e4m3"):
    dtype, down = {"e4m3": (ml_dtypes.float8_e4m3fn, 7), "e5m2": (ml_dtypes.float8_e5m2, 14)}[fmt]
    v = np.moveaxis(np.asarray(x, np.float32).astype(ml_dtypes.bfloat16).astype(np.float64), axis, -1)
    blocks = v.reshape(v.shape[:-1] + (-1, 32))
    amax = np.abs(blocks).max(-1, keepdims=True)
    byte = np.maximum(np.where(amax > 0, np.frexp(amax)[1] - 1 + 127, 0) - down, 1)
    scale = np.exp2(byte - 127.0)
    codes = (blocks / scale).astype(np.float32).astype(dtype).astype(np.float64)
    return np.moveaxis((codes * scale).reshape(v.shape), -1, axis)


WIDE = False


def mx_kscale(k):
    if not WIDE:
        return np.ones(k)
    levels = np.array([10, -10, 5, -5, 0])
    if k % 512:
        return np.exp2(np.random.permutation(np.resize(levels, k // 32))).repeat(32)
    a = np.empty((k // 512, 16))
    for p in range(k // 512):
        a[p, :8] = np.random.permutation(np.resize(levels, 8))
        for g in range(8):
            far = levels[np.abs(levels - a[p, g]) >= 10]
            a[p, g + 8] = far[np.random.randint(len(far))]
    return np.exp2(a.ravel()).repeat(32)


def f64(x):
    return np.asarray(x).astype(np.float64)


def striped(idx):
    return np.tile(idx.reshape(-1, 16).T, (8, 1)).astype(np.uint16)


def unstriped(offs):
    return offs[:16].T.reshape(-1).astype(np.int64)


def pack_weight(w):
    k, n = w.shape
    w = f64(np.asarray(w, np.float32).astype(ml_dtypes.bfloat16)).reshape(k // 32, 32, n)
    amax = np.abs(w).max(1)
    byte = np.clip(np.where(amax > 0, np.frexp(amax)[1] - 1 + 127 - 7, 1), 1, 254)
    scaled = (w * np.exp2(127.0 - byte)[:, None, :]).reshape(k, n).astype(np.float32)
    words = np.ascontiguousarray(scaled.reshape(k // 512, 128, 4, n).transpose(0, 1, 3, 2)).astype(ml_dtypes.float8_e4m3fn).view(np.uint8)
    return words, np.ascontiguousarray(byte.astype(np.uint8).reshape(k // 512, 16, n))


def unpack_weight(words, scales):
    g, p, n, _ = words.shape
    vals = np.ascontiguousarray(words).view(ml_dtypes.float8_e4m3fn).astype(np.float64) * np.repeat(np.exp2(scales.astype(np.float64) - 127.0), 8, axis=1)[..., None]
    return vals.transpose(0, 1, 3, 2).reshape(g * 512, n)


def relu(v):
    return np.maximum(v, 0.0)


K, T, S, V, H, N, J = 512, 2048, 1024, 512, 512, 256, 512


def setup_inputs():
    n = np.random.standard_normal
    s = mx_kscale(K)[:, None]
    u = mx_kscale(H)
    r = mx_kscale(J)[:, None]
    packed_w4 = pack_weight(n((H, N)) / np.sqrt(H) / u[:, None])
    return {
        "xT": (n((K, T)) * s).astype(np.float32),
        "eT": (n((J, V)) * r).astype(np.float32),
        "w1": (n((K, H)) / np.sqrt(3 * K) / s * u).astype(np.float32),
        "w2": (n((K, H)) / np.sqrt(3 * K) / s * u).astype(np.float32),
        "w3": (n((J, H)) / np.sqrt(3 * J) / r * u).astype(np.float32),
        "w4_words": packed_w4[0],
        "w4_scales": packed_w4[1],
        "offs": striped(np.random.permutation(T)[:S]),
    }


def reference(xT, eT, w1, w2, w3, w4_words, w4_scales, offs):
    xq = mxq(f64(xT)[:, unstriped(offs)], 0, "e4m3")
    h = relu(mxq(f64(w1), 0, "e4m3").T @ xq[:, :V] + mxq(f64(w2), 0, "e4m3").T @ xq[:, V:2 * V] + mxq(f64(w3), 0, "e4m3").T @ mxq(f64(eT), 0, "e4m3"))
    return unpack_weight(w4_words, w4_scales).T @ mxq(h, 0, "e4m3")

@@ -1,0 +1,141 @@
+from contextlib import ExitStack
+
+import concourse.mybir as mybir
+
+K, T, S, V, H, N = 512, 2048, 1024, 512, 512, 256
+FLOPS = 2 * V * (3 * K * H + H * N)
+
+F32 = mybir.dt.float32
+BF16 = mybir.dt.bfloat16
+I32 = mybir.dt.int32
+U32 = mybir.dt.uint32
+U16 = mybir.dt.uint16
+U8 = mybir.dt.uint8
+FP8X4 = mybir.dt.float8_e4m3fn_x4
+ACT = mybir.ActivationFunctionType
+
+P = 128
+Q = 128
+NQ = V // Q
+XC = 1024
+X_SPLIT = 704
+W_SPLIT = {1: 0, 2: 64, 3: 88}
+
+
+def tile_picked_edgeup_relu_e_kernel(tc, xT, eT, w1, w2, w3, w4_words, w4_scales, offs, out):
+    nc = tc.nc
+    with ExitStack() as ctx:
+        sb = ctx.enter_context(tc.tile_pool(name="sb", bufs=1))
+        ps = ctx.enter_context(tc.psum_pool(name="ps", bufs=1))
+
+        def tile(shape, dtype, name):
+            return sb.tile(shape, dtype, name=name, align_bytes=64)
+
+        def quantize(src, width, name):
+            codes = tile([P, width], U32, name + "_codes")
+            scales = tile([P, width], U8, name + "_scales")
+            nc.vector.quantize_mx(out=codes[:].bitcast(FP8X4), scales=scales[:], in_=src)
+            return codes, scales
+
+        offsets = sb.tile([P, S // 16], U16, name="offsets")
+
+        x_rows = xT.rearrange("(p u e) t -> p u e t", u=2, e=2)
+        x_raw = {}
+        for u in range(2):
+            for c in range(T // XC):
+                x_raw[u, c] = tile([P, 2, XC], F32, "x_raw%d%d" % (u, c))
+                nc.sync.dma_start(out=x_raw[u, c][:], in_=x_rows[:, u, :, c * XC:(c + 1) * XC])
+                if (u, c) == (0, 0):
+                    nc.sync.dma_start(offsets[:], offs)
+        w_raw = {}
+        for i, w in ((1, w1), (2, w2), (3, w3)):
+            w_raw[i] = tile([P, 4, H], F32, "w_raw%d" % i)
+            nc.sync.dma_start(out=w_raw[i][:], in_=w.rearrange("(p j) c -> p j c", j=4))
+        e_rows = eT.rearrange("(p j) v -> p j v", j=4)
+        e_parts = ((0, 256), (256, 128), (384, 128))
+        e_raw = []
+        for v0, n in e_parts:
+            t_ = tile([P, 4, n], F32, "e_raw%d" % v0)
+            nc.sync.dma_start(out=t_[:], in_=e_rows[:, :, v0:v0 + n])
+            e_raw.append(t_)
+
+        w4_codes = tile([P, N], U32, "w4_codes")
+        w4_sc = tile([P, N], U8, "w4_sc")
+        nc.gpsimd.memset(w4_sc[:], 0)
+        for g in range(4):
+            nc.gpsimd.dma_start(out=w4_sc[32 * g:32 * g + 4, :].bitcast(I32), in_=w4_scales[0, 4 * g:4 * g + 4, :].bitcast(I32))
+        nc.gpsimd.dma_start(out=w4_codes[:].bitcast(I32), in_=w4_words[0].rearrange("p n t -> p (n t)").bitcast(I32))
+
+        picked = [tile([P, V, 4], BF16, "picked%d" % s) for s in range(2)]
+        for u in range(2):
+            pairs = tile([P, T, 2], BF16, "pairs%d" % u)
+            for c in range(T // XC):
+                src = x_raw[u, c][:].rearrange("p e n -> p n e")
+                dst = pairs[:, c * XC:(c + 1) * XC, :]
+                nv = X_SPLIT if c == 1 else (XC if u == 0 else 0)
+                if nv > 0:
+                    nc.vector.tensor_copy(out=dst[:, :nv, :], in_=src[:, :nv, :])
+                if nv < XC:
+                    nc.scalar.activation(out=dst[:, nv:, :], in_=src[:, nv:, :], func=ACT.Copy)
+            window = pairs[:].rearrange("p n e -> p (n e)").bitcast(U32)
+            for s in range(2):
+                words = picked[s][:].rearrange("p v j -> p (v j)").bitcast(U32).rearrange("p (v u) -> p v u", u=2)
+                nc.vector.tensor_copy(out=words[:, :, u], in_=window.indirect(offsets[:, s * (V // 16):(s + 1) * (V // 16)]))
+        xq = [quantize(picked[s][:].rearrange("p v j -> p (v j)"), V, "x%d" % s) for s in range(2)]
+
+        banks = [ps.tile([P, 4, Q], F32, name="h_acc%d" % q) for q in range(NQ)]
+
+        def weights(i):
+            wb = tile([P, 4, P, 4], BF16, "w_bf%d" % i)
+            dst = wb[:].rearrange("p t m j -> p m j t")
+            src = w_raw[i][:].rearrange("p j (m t) -> p m j t", t=4)
+            nv = W_SPLIT[i]
+            if nv > 0:
+                nc.vector.tensor_copy(out=dst[:, :nv], in_=src[:, :nv])
+            nc.scalar.copy(out=dst[:, nv:], in_=src[:, nv:])
+            return quantize(wb[:].rearrange("p t m j -> p (t m j)"), H, "w%d" % i)
+
+        def passes(q, wq, aq, col0, start, stop):
+            for t in range(4):
+                nc.tensor.matmul_mx(
+                    out=banks[q][:, t, :],
+                    lhsT=wq[0][:, t * P:(t + 1) * P].bitcast(FP8X4), lhsT_scale=wq[1][:, t * P:(t + 1) * P],
+                    rhs=aq[0][:, col0:col0 + Q].bitcast(FP8X4), rhs_scale=aq[1][:, col0:col0 + Q],
+                    start=(start and t == 0), stop=(stop and t == 3))
+
+        w1q = weights(1)
+        for q in range(NQ):
+            passes(q, w1q, xq[0], q * Q, True, False)
+        w2q = weights(2)
+        for q in range(NQ):
+            passes(q, w2q, xq[1], q * Q, False, False)
+        w3q = weights(3)
+
+        out_rows = out.rearrange("(a p) v -> p a v", p=P)
+
+        def finish(q):
+            hb = tile([P, Q, 4], BF16, "h_bf%d" % q)
+            nc.scalar.activation(out=hb[:], in_=banks[q][:].rearrange("p t v -> p v t"), func=ACT.Relu)
+            hq = quantize(hb[:].rearrange("p v t -> p (v t)"), Q, "h%d" % q)
+            acc = ps.tile([P, 2, Q], F32, name="o_acc%d" % q)
+            for a in range(2):
+                nc.tensor.matmul_mx(
+                    out=acc[:, a, :],
+                    lhsT=w4_codes[:, a * P:(a + 1) * P].bitcast(FP8X4), lhsT_scale=w4_sc[:, a * P:(a + 1) * P],
+                    rhs=hq[0][:].bitcast(FP8X4), rhs_scale=hq[1][:], start=True, stop=True)
+            res = tile([P, 2, Q], F32, "res%d" % q)
+            if q < 2:
+                nc.scalar.copy(out=res[:], in_=acc[:])
+            else:
+                nc.vector.tensor_copy(out=res[:], in_=acc[:])
+            nc.sync.dma_start(out=out_rows[:, :, q * Q:(q + 1) * Q], in_=res[:])
+
+        for part, (v0, n) in enumerate(e_parts):
+            eb = tile([P, n, 4], BF16, "e_bf%d" % v0)
+            nc.vector.tensor_copy(out=eb[:].rearrange("p (c i) j -> p c j i", i=4),
+                                  in_=e_raw[part][:].rearrange("p j (c i) -> p c j i", i=4))
+            eq = quantize(eb[:].rearrange("p v j -> p (v j)"), n, "e%d" % v0)
+            for q in range(v0 // Q, (v0 + n) // Q):
+                passes(q, w3q, eq, q * Q - v0, False, True)
+        for q in range(NQ):
+            finish(q)

@@ -17,9 +17,9 @@ ACT = mybir.ActivationFunctionType
 P = 128
 Q = 128
 NQ = V // Q
-XC = 1024
-X_SPLIT = 704
-W_SPLIT = {1: 0, 2: 64, 3: 88}
+X_CHUNKS = ((0, 1024), (1024, 512), (1536, 512))
+X_SPLIT = 352
+W_SPLIT = 44
 
 
 def tile_picked_edgeup_relu_e_kernel(tc, xT, eT, w1, w2, w3, w4_words, w4_scales, offs, out):
@@ -31,8 +31,8 @@ def tile_picked_edgeup_relu_e_kernel(tc, xT, eT, w1, w2, w3, w4_words, w4_scales
         def tile(shape, dtype, name):
             return sb.tile(shape, dtype, name=name, align_bytes=64)
 
-        def quantize(src, width, name):
-            codes = tile([P, width], U32, name + "_codes")
+        def quantize(src, width, name, tag=None):
+            codes = sb.tile([P, width], U32, name=name + "_codes", tag=tag or name + "_codes", align_bytes=64)
             scales = tile([P, width], U8, name + "_scales")
             nc.vector.quantize_mx(out=codes[:].bitcast(FP8X4), scales=scales[:], in_=src)
             return codes, scales
@@ -42,57 +42,64 @@ def tile_picked_edgeup_relu_e_kernel(tc, xT, eT, w1, w2, w3, w4_words, w4_scales
         x_rows = xT.rearrange("(p u e) t -> p u e t", u=2, e=2)
         x_raw = {}
         for u in range(2):
-            for c in range(T // XC):
-                x_raw[u, c] = tile([P, 2, XC], F32, "x_raw%d%d" % (u, c))
-                nc.sync.dma_start(out=x_raw[u, c][:], in_=x_rows[:, u, :, c * XC:(c + 1) * XC])
+            for c, (n0, n) in enumerate(X_CHUNKS):
+                x_raw[u, c] = tile([P, 2, n], F32, "x_raw%d%d" % (u, c))
+                nc.sync.dma_start(out=x_raw[u, c][:], in_=x_rows[:, u, :, n0:n0 + n])
                 if (u, c) == (0, 0):
                     nc.sync.dma_start(offsets[:], offs)
         w_raw = {}
-        for i, w in ((1, w1), (2, w2), (3, w3)):
-            w_raw[i] = tile([P, 4, H], F32, "w_raw%d" % i)
-            nc.sync.dma_start(out=w_raw[i][:], in_=w.rearrange("(p j) c -> p j c", j=4))
-        e_rows = eT.rearrange("(p j) v -> p j v", j=4)
-        e_parts = ((0, 256), (256, 128), (384, 128))
-        e_raw = []
-        for v0, n in e_parts:
-            t_ = tile([P, 4, n], F32, "e_raw%d" % v0)
-            nc.sync.dma_start(out=t_[:], in_=e_rows[:, :, v0:v0 + n])
-            e_raw.append(t_)
+        e_raw = {}
+
+        def load_w(i, w):
+            for half in range(2):
+                w_raw[i, half] = tile([P, 4, H // 2], F32, "w_raw%d%d" % (i, half))
+                nc.sync.dma_start(out=w_raw[i, half][:], in_=w.rearrange("(p j) c -> p j c", j=4)[:, :, half * 256:(half + 1) * 256])
+
+        def load_e(q):
+            e_raw[q] = tile([P, 4, Q], F32, "e_raw%d" % q)
+            nc.sync.dma_start(out=e_raw[q][:], in_=eT.rearrange("(p j) v -> p j v", j=4)[:, :, q * Q:(q + 1) * Q])
+
+        load_w(1, w1)
+        load_e(0)
+        load_w(2, w2)
+        load_w(3, w3)
+        for q in range(1, NQ):
+            load_e(q)
 
         w4_codes = tile([P, N], U32, "w4_codes")
         w4_sc = tile([P, N], U8, "w4_sc")
-        nc.gpsimd.memset(w4_sc[:], 0)
+        nc.vector.memset(w4_sc[:].bitcast(I32), 0)
+        nc.sync.dma_start(out=w4_codes[:].bitcast(I32), in_=w4_words[0].rearrange("p n t -> p (n t)").bitcast(I32))
         for g in range(4):
-            nc.gpsimd.dma_start(out=w4_sc[32 * g:32 * g + 4, :].bitcast(I32), in_=w4_scales[0, 4 * g:4 * g + 4, :].bitcast(I32))
-        nc.gpsimd.dma_start(out=w4_codes[:].bitcast(I32), in_=w4_words[0].rearrange("p n t -> p (n t)").bitcast(I32))
+            nc.sync.dma_start(out=w4_sc[32 * g:32 * g + 4, :].bitcast(I32), in_=w4_scales[0, 4 * g:4 * g + 4, :].bitcast(I32))
 
         picked = [tile([P, V, 4], BF16, "picked%d" % s) for s in range(2)]
         for u in range(2):
             pairs = tile([P, T, 2], BF16, "pairs%d" % u)
-            for c in range(T // XC):
+            for c, (n0, n) in enumerate(X_CHUNKS):
                 src = x_raw[u, c][:].rearrange("p e n -> p n e")
-                dst = pairs[:, c * XC:(c + 1) * XC, :]
-                nv = X_SPLIT if c == 1 else (XC if u == 0 else 0)
+                dst = pairs[:, n0:n0 + n, :]
+                nv = X_SPLIT if c == 2 else (0 if (u, c) == (1, 0) else n)
                 if nv > 0:
                     nc.vector.tensor_copy(out=dst[:, :nv, :], in_=src[:, :nv, :])
-                if nv < XC:
+                if nv < n:
                     nc.scalar.activation(out=dst[:, nv:, :], in_=src[:, nv:, :], func=ACT.Copy)
             window = pairs[:].rearrange("p n e -> p (n e)").bitcast(U32)
             for s in range(2):
                 words = picked[s][:].rearrange("p v j -> p (v j)").bitcast(U32).rearrange("p (v u) -> p v u", u=2)
                 nc.vector.tensor_copy(out=words[:, :, u], in_=window.indirect(offsets[:, s * (V // 16):(s + 1) * (V // 16)]))
-        xq = [quantize(picked[s][:].rearrange("p v j -> p (v j)"), V, "x%d" % s) for s in range(2)]
 
-        banks = [ps.tile([P, 4, Q], F32, name="h_acc%d" % q) for q in range(NQ)]
+        banks = [ps.tile([P, 4, Q], F32, name="h_acc%d" % q, tag="bank%d" % q) for q in range(NQ)]
 
-        def weights(i):
-            wb = tile([P, 4, P, 4], BF16, "w_bf%d" % i)
-            dst = wb[:].rearrange("p t m j -> p m j t")
-            src = w_raw[i][:].rearrange("p j (m t) -> p m j t", t=4)
-            nv = W_SPLIT[i]
-            if nv > 0:
-                nc.vector.tensor_copy(out=dst[:, :nv], in_=src[:, :nv])
-            nc.scalar.copy(out=dst[:, nv:], in_=src[:, nv:])
+        def weights(i, shares):
+            wb = sb.tile([P, 4, P, 4], BF16, name="w_bf%d" % i, tag="w_bf%d" % i, align_bytes=64)
+            for half, nv in enumerate(shares):
+                dst = wb[:, :, half * 64:(half + 1) * 64, :].rearrange("p t m j -> p m j t")
+                src = w_raw[i, half][:].rearrange("p j (m t) -> p m j t", t=4)
+                if nv > 0:
+                    nc.vector.tensor_copy(out=dst[:, :nv], in_=src[:, :nv])
+                if nv < 64:
+                    nc.scalar.copy(out=dst[:, nv:], in_=src[:, nv:])
             return quantize(wb[:].rearrange("p t m j -> p (t m j)"), H, "w%d" % i)
 
         def passes(q, wq, aq, col0, start, stop):
@@ -103,39 +110,66 @@ def tile_picked_edgeup_relu_e_kernel(tc, xT, eT, w1, w2, w3, w4_words, w4_scales
                     rhs=aq[0][:, col0:col0 + Q].bitcast(FP8X4), rhs_scale=aq[1][:, col0:col0 + Q],
                     start=(start and t == 0), stop=(stop and t == 3))
 
-        w1q = weights(1)
+        def edges_cast(q, on_vector):
+            eb = tile([P, Q, 4], BF16, "e_bf%d" % q)
+            dst = eb[:].rearrange("p (c i) j -> p c j i", i=4)
+            src = e_raw[q][:].rearrange("p j (c i) -> p c j i", i=4)
+            if on_vector:
+                nc.vector.tensor_copy(out=dst, in_=src)
+            else:
+                nc.scalar.copy(out=dst, in_=src)
+            return eb
+
+        def edges_quant(q, eb):
+            return quantize(eb[:].rearrange("p v j -> p (v j)"), Q, "e%d" % q)
+
+        xs = quantize(picked[0][:].rearrange("p v j -> p (v j)"), V, "x0")
+        w1q = weights(1, (0, 0))
         for q in range(NQ):
-            passes(q, w1q, xq[0], q * Q, True, False)
-        w2q = weights(2)
+            passes(q, w1q, xs, q * Q, True, False)
+        xd = quantize(picked[1][:].rearrange("p v j -> p (v j)"), V, "x1", tag="w_bf1")
+        eq = {0: edges_quant(0, edges_cast(0, False))}
+        w2q = weights(2, (0, 0))
         for q in range(NQ):
-            passes(q, w2q, xq[1], q * Q, False, False)
-        w3q = weights(3)
+            passes(q, w2q, xd, q * Q, False, False)
+        w3q = weights(3, (64, W_SPLIT))
+        ebs = {q: edges_cast(q, q == 3) for q in range(1, NQ)}
+        passes(0, w3q, eq[0], 0, False, True)
+        for q in range(1, NQ):
+            eq[q] = edges_quant(q, ebs[q])
+            passes(q, w3q, eq[q], 0, False, True)
 
         out_rows = out.rearrange("(a p) v -> p a v", p=P)
 
-        def finish(q):
+        def second(a, hq, acc):
+            nc.tensor.matmul_mx(
+                out=acc,
+                lhsT=w4_codes[:, a * P:(a + 1) * P].bitcast(FP8X4), lhsT_scale=w4_sc[:, a * P:(a + 1) * P],
+                rhs=hq[0][:].bitcast(FP8X4), rhs_scale=hq[1][:], start=True, stop=True)
+
+        hqs = {}
+        for q in range(NQ):
             hb = tile([P, Q, 4], BF16, "h_bf%d" % q)
-            nc.scalar.activation(out=hb[:], in_=banks[q][:].rearrange("p t v -> p v t"), func=ACT.Relu)
-            hq = quantize(hb[:].rearrange("p v t -> p (v t)"), Q, "h%d" % q)
-            acc = ps.tile([P, 2, Q], F32, name="o_acc%d" % q)
+            if q == 2:
+                nc.vector.tensor_scalar_max(out=hb[:], in0=banks[q][:].rearrange("p t v -> p v t"), scalar1=0.0)
+            else:
+                nc.scalar.activation(out=hb[:], in_=banks[q][:].rearrange("p t v -> p v t"), func=ACT.Relu)
+            hqs[q] = quantize(hb[:].rearrange("p v t -> p (v t)"), Q, "h%d" % q)
+        for q in range(NQ - 1):
+            acc = ps.tile([P, 2, Q], F32, name="o_acc%d" % q, tag="bank%d" % (4 + q))
             for a in range(2):
-                nc.tensor.matmul_mx(
-                    out=acc[:, a, :],
-                    lhsT=w4_codes[:, a * P:(a + 1) * P].bitcast(FP8X4), lhsT_scale=w4_sc[:, a * P:(a + 1) * P],
-                    rhs=hq[0][:].bitcast(FP8X4), rhs_scale=hq[1][:], start=True, stop=True)
+                second(a, hqs[q], acc[:, a, :])
             res = tile([P, 2, Q], F32, "res%d" % q)
-            if q < 2:
+            nc.scalar.copy(out=res[:], in_=acc[:])
+            nc.sync.dma_start(out=out_rows[:, :, q * Q:(q + 1) * Q], in_=res[:])
+        q = NQ - 1
+        for a in range(2):
+            acc = ps.tile([P, Q], F32, name="o_last%d" % a, tag="bank%d" % (7 if a == 0 else 0))
+            second(a, hqs[q], acc[:])
+            res = tile([P, Q], F32, "res_last%d" % a)
+            if a == 0:
                 nc.scalar.copy(out=res[:], in_=acc[:])
+                nc.scalar.dma_start(out=out_rows[:, a, q * Q:(q + 1) * Q], in_=res[:])
             else:
                 nc.vector.tensor_copy(out=res[:], in_=acc[:])
-            nc.sync.dma_start(out=out_rows[:, :, q * Q:(q + 1) * Q], in_=res[:])
-
-        for part, (v0, n) in enumerate(e_parts):
-            eb = tile([P, n, 4], BF16, "e_bf%d" % v0)
-            nc.vector.tensor_copy(out=eb[:].rearrange("p (c i) j -> p c j i", i=4),
-                                  in_=e_raw[part][:].rearrange("p j (c i) -> p c j i", i=4))
-            eq = quantize(eb[:].rearrange("p v j -> p (v j)"), n, "e%d" % v0)
-            for q in range(v0 // Q, (v0 + n) // Q):
-                passes(q, w3q, eq, q * Q - v0, False, True)
-        for q in range(NQ):
-            finish(q)
+                nc.sync.dma_start(out=out_rows[:, a, q * Q:(q + 1) * Q], in_=res[:])

@@ -17,9 +17,8 @@ ACT = mybir.ActivationFunctionType
 P = 128
 Q = 128
 NQ = V // Q
-X_CHUNKS = ((0, 1024), (1024, 512), (1536, 512))
-X_SPLIT = 352
-W_SPLIT = 44
+X_CHUNKS = (((0, 1280, 1280), (1280, 768, 520)), ((0, 1024, 0), (1024, 512, 512), (1536, 512, 352)))
+WEAVE_SPLIT = (512, 0)
 
 
 def tile_picked_edgeup_relu_e_kernel(tc, xT, eT, w1, w2, w3, w4_words, w4_scales, offs, out):
@@ -42,7 +41,7 @@ def tile_picked_edgeup_relu_e_kernel(tc, xT, eT, w1, w2, w3, w4_words, w4_scales
         x_rows = xT.rearrange("(p u e) t -> p u e t", u=2, e=2)
         x_raw = {}
         for u in range(2):
-            for c, (n0, n) in enumerate(X_CHUNKS):
+            for c, (n0, n, nv) in enumerate(X_CHUNKS[u]):
                 x_raw[u, c] = tile([P, 2, n], F32, "x_raw%d%d" % (u, c))
                 nc.sync.dma_start(out=x_raw[u, c][:], in_=x_rows[:, u, :, n0:n0 + n])
                 if (u, c) == (0, 0):
@@ -50,21 +49,24 @@ def tile_picked_edgeup_relu_e_kernel(tc, xT, eT, w1, w2, w3, w4_words, w4_scales
         w_raw = {}
         e_raw = {}
 
-        def load_w(i, w):
-            for half in range(2):
-                w_raw[i, half] = tile([P, 4, H // 2], F32, "w_raw%d%d" % (i, half))
-                nc.sync.dma_start(out=w_raw[i, half][:], in_=w.rearrange("(p j) c -> p j c", j=4)[:, :, half * 256:(half + 1) * 256])
+        def load_w(i, w, parts):
+            n = H // parts
+            for part in range(parts):
+                w_raw[i, part] = tile([P, 4, n], F32, "w_raw%d%d" % (i, part))
+                nc.sync.dma_start(out=w_raw[i, part][:], in_=w.rearrange("(p j) c -> p j c", j=4)[:, :, part * n:(part + 1) * n])
 
-        def load_e(q):
-            e_raw[q] = tile([P, 4, Q], F32, "e_raw%d" % q)
-            nc.sync.dma_start(out=e_raw[q][:], in_=eT.rearrange("(p j) v -> p j v", j=4)[:, :, q * Q:(q + 1) * Q])
+        def load_e(q0, nq):
+            raw = tile([P, 4, nq * Q], F32, "e_raw%d" % q0)
+            nc.sync.dma_start(out=raw[:], in_=eT.rearrange("(p j) v -> p j v", j=4)[:, :, q0 * Q:(q0 + nq) * Q])
+            for q in range(nq):
+                e_raw[q0 + q] = raw[:, :, q * Q:(q + 1) * Q]
 
-        load_w(1, w1)
-        load_e(0)
-        load_w(2, w2)
-        load_w(3, w3)
-        for q in range(1, NQ):
-            load_e(q)
+        load_w(1, w1, 2)
+        load_w(2, w2, 1)
+        load_w(3, w3, 1)
+        load_e(0, 2)
+        load_e(2, 1)
+        load_e(3, 1)
 
         w4_codes = tile([P, N], U32, "w4_codes")
         w4_sc = tile([P, N], U8, "w4_sc")
@@ -73,32 +75,43 @@ def tile_picked_edgeup_relu_e_kernel(tc, xT, eT, w1, w2, w3, w4_words, w4_scales
         for g in range(4):
             nc.sync.dma_start(out=w4_sc[32 * g:32 * g + 4, :].bitcast(I32), in_=w4_scales[0, 4 * g:4 * g + 4, :].bitcast(I32))
 
-        picked = [tile([P, V, 4], BF16, "picked%d" % s) for s in range(2)]
+        picked = [tile([P, V, 4], BF16, "picked0"), sb.tile([P, V, 4], BF16, name="picked1", tag="w_raw11", align_bytes=64)]
+        gathered = [tile([P, 2, V], I32, "gathered%d" % s) for s in range(2)]
         for u in range(2):
             pairs = tile([P, T, 2], BF16, "pairs%d" % u)
-            for c, (n0, n) in enumerate(X_CHUNKS):
+            for c, (n0, n, nv) in enumerate(X_CHUNKS[u]):
                 src = x_raw[u, c][:].rearrange("p e n -> p n e")
                 dst = pairs[:, n0:n0 + n, :]
-                nv = X_SPLIT if c == 2 else (0 if (u, c) == (1, 0) else n)
                 if nv > 0:
                     nc.vector.tensor_copy(out=dst[:, :nv, :], in_=src[:, :nv, :])
                 if nv < n:
                     nc.scalar.activation(out=dst[:, nv:, :], in_=src[:, nv:, :], func=ACT.Copy)
             window = pairs[:].rearrange("p n e -> p (n e)").bitcast(U32)
             for s in range(2):
-                words = picked[s][:].rearrange("p v j -> p (v j)").bitcast(U32).rearrange("p (v u) -> p v u", u=2)
-                nc.vector.tensor_copy(out=words[:, :, u], in_=window.indirect(offsets[:, s * (V // 16):(s + 1) * (V // 16)]))
+                nc.vector.tensor_copy(out=gathered[s][:, u, :].bitcast(U32),
+                                      in_=window.indirect(offsets[:, s * (V // 16):(s + 1) * (V // 16)]))
+        for s in range(2):
+            nv = WEAVE_SPLIT[s]
+            words = picked[s][:].rearrange("p v j -> p (v j)")
+            src = gathered[s][:]
+            if nv > 0:
+                nc.vector.tensor_copy(out=words.bitcast(I32).rearrange("p (v u) -> p v u", u=2)[:, :nv, :],
+                                  in_=src.rearrange("p u v -> p v u")[:, :nv, :])
+            if nv < V:
+                nc.scalar.copy(out=words.bitcast(U32).rearrange("p (v u) -> p v u", u=2)[:, nv:, :],
+                               in_=src.bitcast(U32).rearrange("p u v -> p v u")[:, nv:, :])
 
         banks = [ps.tile([P, 4, Q], F32, name="h_acc%d" % q, tag="bank%d" % q) for q in range(NQ)]
 
         def weights(i, shares):
             wb = sb.tile([P, 4, P, 4], BF16, name="w_bf%d" % i, tag="w_bf%d" % i, align_bytes=64)
+            n = P // len(shares)
             for half, nv in enumerate(shares):
-                dst = wb[:, :, half * 64:(half + 1) * 64, :].rearrange("p t m j -> p m j t")
+                dst = wb[:, :, half * n:(half + 1) * n, :].rearrange("p t m j -> p m j t")
                 src = w_raw[i, half][:].rearrange("p j (m t) -> p m j t", t=4)
                 if nv > 0:
                     nc.vector.tensor_copy(out=dst[:, :nv], in_=src[:, :nv])
-                if nv < 64:
+                if nv < n:
                     nc.scalar.copy(out=dst[:, nv:], in_=src[:, nv:])
             return quantize(wb[:].rearrange("p t m j -> p (t m j)"), H, "w%d" % i)
 
@@ -110,12 +123,12 @@ def tile_picked_edgeup_relu_e_kernel(tc, xT, eT, w1, w2, w3, w4_words, w4_scales
                     rhs=aq[0][:, col0:col0 + Q].bitcast(FP8X4), rhs_scale=aq[1][:, col0:col0 + Q],
                     start=(start and t == 0), stop=(stop and t == 3))
 
-        def edges_cast(q, on_vector):
+        def edges_cast(q, nv):
             eb = tile([P, Q, 4], BF16, "e_bf%d" % q)
             dst = eb[:].rearrange("p (c i) j -> p c j i", i=4)
-            src = e_raw[q][:].rearrange("p j (c i) -> p c j i", i=4)
-            if on_vector:
-                nc.vector.tensor_copy(out=dst, in_=src)
+            src = e_raw[q].rearrange("p j (c i) -> p c j i", i=4)
+            if nv > 0:
+                nc.vector.tensor_copy(out=dst[:, :nv], in_=src[:, :nv])
             else:
                 nc.scalar.copy(out=dst, in_=src)
             return eb
@@ -127,15 +140,14 @@ def tile_picked_edgeup_relu_e_kernel(tc, xT, eT, w1, w2, w3, w4_words, w4_scales
         w1q = weights(1, (0, 0))
         for q in range(NQ):
             passes(q, w1q, xs, q * Q, True, False)
-        xd = quantize(picked[1][:].rearrange("p v j -> p (v j)"), V, "x1", tag="w_bf1")
-        eq = {0: edges_quant(0, edges_cast(0, False))}
-        w2q = weights(2, (0, 0))
+        xd = quantize(picked[1][:].rearrange("p v j -> p (v j)"), V, "x1")
+        eq = {}
+        w2q = weights(2, (48,))
         for q in range(NQ):
             passes(q, w2q, xd, q * Q, False, False)
-        w3q = weights(3, (64, W_SPLIT))
-        ebs = {q: edges_cast(q, q == 3) for q in range(1, NQ)}
-        passes(0, w3q, eq[0], 0, False, True)
-        for q in range(1, NQ):
+        w3q = weights(3, (72,))
+        ebs = {q: edges_cast(q, 32 * (q % 2)) for q in range(NQ)}
+        for q in range(NQ):
             eq[q] = edges_quant(q, ebs[q])
             passes(q, w3q, eq[q], 0, False, True)
 
@@ -150,7 +162,7 @@ def tile_picked_edgeup_relu_e_kernel(tc, xT, eT, w1, w2, w3, w4_words, w4_scales
         hqs = {}
         for q in range(NQ):
             hb = tile([P, Q, 4], BF16, "h_bf%d" % q)
-            if q == 2:
+            if q == 1:
                 nc.vector.tensor_scalar_max(out=hb[:], in0=banks[q][:].rearrange("p t v -> p v t"), scalar1=0.0)
             else:
                 nc.scalar.activation(out=hb[:], in_=banks[q][:].rearrange("p t v -> p v t"), func=ACT.Relu)

@@ -107,12 +107,11 @@ def tile_picked_edgeup_relu_e_kernel(tc, xT, eT, w1, w2, w3, w4_words, w4_scales
             wb = sb.tile([P, 4, P, 4], BF16, name="w_bf%d" % i, tag="w_bf%d" % i, align_bytes=64)
             n = P // len(shares)
             for half, nv in enumerate(shares):
-                dst = wb[:, :, half * n:(half + 1) * n, :].rearrange("p t m j -> p m j t")
-                src = w_raw[i, half][:].rearrange("p j (m t) -> p m j t", t=4)
+                dst = wb[:, :, half * n:(half + 1) * n, :].rearrange("p t (b m) j -> p b j m t", m=2)
+                src = w_raw[i, half][:].rearrange("p j (b m t) -> p b j m t", m=2, t=4)
                 if nv > 0:
-                    nc.vector.tensor_copy(out=dst[:, :nv], in_=src[:, :nv])
-                if nv < n:
-                    nc.scalar.copy(out=dst[:, nv:], in_=src[:, nv:])
+                    nc.vector.tensor_copy(out=dst[:, :nv // 2], in_=src[:, :nv // 2])
+                nc.scalar.copy(out=dst[:, nv // 2:], in_=src[:, nv // 2:])
             return quantize(wb[:].rearrange("p t m j -> p (t m j)"), H, "w%d" % i)
 
         def passes(q, wq, aq, col0, start, stop):

@@ -17,8 +17,8 @@ ACT = mybir.ActivationFunctionType
 P = 128
 Q = 128
 NQ = V // Q
-X_CHUNKS = (((0, 1280, 1280), (1280, 768, 520)), ((0, 1024, 0), (1024, 512, 512), (1536, 512, 352)))
-WEAVE_SPLIT = (512, 0)
+NV = 640
+FIRST_V = 256
 
 
 def tile_picked_edgeup_relu_e_kernel(tc, xT, eT, w1, w2, w3, w4_words, w4_scales, offs, out):
@@ -38,14 +38,12 @@ def tile_picked_edgeup_relu_e_kernel(tc, xT, eT, w1, w2, w3, w4_words, w4_scales
 
         offsets = sb.tile([P, S // 16], U16, name="offsets")
 
-        x_rows = xT.rearrange("(p u e) t -> p u e t", u=2, e=2)
-        x_raw = {}
-        for u in range(2):
-            for c, (n0, n, nv) in enumerate(X_CHUNKS[u]):
-                x_raw[u, c] = tile([P, 2, n], F32, "x_raw%d%d" % (u, c))
-                nc.sync.dma_start(out=x_raw[u, c][:], in_=x_rows[:, u, :, n0:n0 + n])
-                if (u, c) == (0, 0):
-                    nc.sync.dma_start(offsets[:], offs)
+        nc.sync.dma_start(offsets[:], offs)
+        x_rows = xT.rearrange("(p j) t -> p j t", j=4)
+        x_raw = []
+        for j in range(4):
+            x_raw.append(tile([P, T], F32, "x_raw%d" % j))
+            nc.sync.dma_start(out=x_raw[j][:], in_=x_rows[:, j, :])
         w_raw = {}
         e_raw = {}
 
@@ -61,7 +59,7 @@ def tile_picked_edgeup_relu_e_kernel(tc, xT, eT, w1, w2, w3, w4_words, w4_scales
             for q in range(nq):
                 e_raw[q0 + q] = raw[:, :, q * Q:(q + 1) * Q]
 
-        load_w(1, w1, 2)
+        load_w(1, w1, 1)
         load_w(2, w2, 1)
         load_w(3, w3, 1)
         load_e(0, 2)
@@ -75,43 +73,30 @@ def tile_picked_edgeup_relu_e_kernel(tc, xT, eT, w1, w2, w3, w4_words, w4_scales
         for g in range(4):
             nc.sync.dma_start(out=w4_sc[32 * g:32 * g + 4, :].bitcast(I32), in_=w4_scales[0, 4 * g:4 * g + 4, :].bitcast(I32))
 
-        picked = [tile([P, V, 4], BF16, "picked0"), sb.tile([P, V, 4], BF16, name="picked1", tag="w_raw11", align_bytes=64)]
-        gathered = [tile([P, 2, V], I32, "gathered%d" % s) for s in range(2)]
+        picked = tile([P, S, 4], BF16, "picked")
         for u in range(2):
-            pairs = tile([P, T, 2], BF16, "pairs%d" % u)
-            for c, (n0, n, nv) in enumerate(X_CHUNKS[u]):
-                src = x_raw[u, c][:].rearrange("p e n -> p n e")
-                dst = pairs[:, n0:n0 + n, :]
+            gathered = tile([P, 2, S - NV], BF16, "gathered%d" % u)
+            for e in range(2):
+                j = 2 * u + e
+                nc.vector.tensor_copy(out=picked[:, :NV, j], in_=x_raw[j][:].indirect(offsets[:, :NV // 16]))
+                nv = FIRST_V if j == 0 else 0
                 if nv > 0:
-                    nc.vector.tensor_copy(out=dst[:, :nv, :], in_=src[:, :nv, :])
-                if nv < n:
-                    nc.scalar.activation(out=dst[:, nv:, :], in_=src[:, nv:, :], func=ACT.Copy)
-            window = pairs[:].rearrange("p n e -> p (n e)").bitcast(U32)
-            for s in range(2):
-                nc.vector.tensor_copy(out=gathered[s][:, u, :].bitcast(U32),
-                                      in_=window.indirect(offsets[:, s * (V // 16):(s + 1) * (V // 16)]))
-        for s in range(2):
-            nv = WEAVE_SPLIT[s]
-            words = picked[s][:].rearrange("p v j -> p (v j)")
-            src = gathered[s][:]
-            if nv > 0:
-                nc.vector.tensor_copy(out=words.bitcast(I32).rearrange("p (v u) -> p v u", u=2)[:, :nv, :],
-                                  in_=src.rearrange("p u v -> p v u")[:, :nv, :])
-            if nv < V:
-                nc.scalar.copy(out=words.bitcast(U32).rearrange("p (v u) -> p v u", u=2)[:, nv:, :],
-                               in_=src.bitcast(U32).rearrange("p u v -> p v u")[:, nv:, :])
+                    nc.vector.tensor_copy(out=gathered[:, e, :nv], in_=x_raw[j][:].indirect(offsets[:, NV // 16:(NV + nv) // 16]))
+                nc.scalar.activation(out=gathered[:, e, nv:], in_=x_raw[j][:].indirect(offsets[:, (NV + nv) // 16:]), func=ACT.Copy)
+            nc.scalar.copy(out=picked[:, NV:, 2 * u:2 * u + 2], in_=gathered[:].rearrange("p e v -> p v e"))
 
         banks = [ps.tile([P, 4, Q], F32, name="h_acc%d" % q, tag="bank%d" % q) for q in range(NQ)]
 
         def weights(i, shares):
-            wb = sb.tile([P, 4, P, 4], BF16, name="w_bf%d" % i, tag="w_bf%d" % i, align_bytes=64)
+            wb = sb.tile([P, 4, P, 4], BF16, name="w_bf%d" % i, tag="w_bf", align_bytes=64)
             n = P // len(shares)
             for half, nv in enumerate(shares):
                 dst = wb[:, :, half * n:(half + 1) * n, :].rearrange("p t (b m) j -> p b j m t", m=2)
                 src = w_raw[i, half][:].rearrange("p j (b m t) -> p b j m t", m=2, t=4)
                 if nv > 0:
                     nc.vector.tensor_copy(out=dst[:, :nv // 2], in_=src[:, :nv // 2])
-                nc.scalar.copy(out=dst[:, nv // 2:], in_=src[:, nv // 2:])
+                if nv < n:
+                    nc.scalar.copy(out=dst[:, nv // 2:], in_=src[:, nv // 2:])
             return quantize(wb[:].rearrange("p t m j -> p (t m j)"), H, "w%d" % i)
 
         def passes(q, wq, aq, col0, start, stop):
@@ -135,16 +120,16 @@ def tile_picked_edgeup_relu_e_kernel(tc, xT, eT, w1, w2, w3, w4_words, w4_scales
         def edges_quant(q, eb):
             return quantize(eb[:].rearrange("p v j -> p (v j)"), Q, "e%d" % q)
 
-        xs = quantize(picked[0][:].rearrange("p v j -> p (v j)"), V, "x0")
-        w1q = weights(1, (0, 0))
+        xs = quantize(picked[:, :V, :].rearrange("p v j -> p (v j)"), V, "x0")
+        w1q = weights(1, (72,))
+        xd = quantize(picked[:, V:, :].rearrange("p v j -> p (v j)"), V, "x1", tag="w_raw10")
         for q in range(NQ):
             passes(q, w1q, xs, q * Q, True, False)
-        xd = quantize(picked[1][:].rearrange("p v j -> p (v j)"), V, "x1")
         eq = {}
-        w2q = weights(2, (48,))
+        w2q = weights(2, (60,))
         for q in range(NQ):
             passes(q, w2q, xd, q * Q, False, False)
-        w3q = weights(3, (72,))
+        w3q = weights(3, (84,))
         ebs = {q: edges_cast(q, 32 * (q % 2)) for q in range(NQ)}
         for q in range(NQ):
             eq[q] = edges_quant(q, ebs[q])

@@ -25,25 +25,28 @@ def tile_picked_edgeup_relu_e_kernel(tc, xT, eT, w1, w2, w3, w4_words, w4_scales
     nc = tc.nc
     with ExitStack() as ctx:
         sb = ctx.enter_context(tc.tile_pool(name="sb", bufs=1))
+        late = ctx.enter_context(tc.tile_pool(name="late", bufs=1))
         ps = ctx.enter_context(tc.psum_pool(name="ps", bufs=1))
 
         def tile(shape, dtype, name):
             return sb.tile(shape, dtype, name=name, align_bytes=64)
 
-        def quantize(src, width, name, tag=None):
-            codes = sb.tile([P, width], U32, name=name + "_codes", tag=tag or name + "_codes", align_bytes=64)
+        def quantize(src, width, name, tag=None, codes=None):
+            if codes is None:
+                codes = sb.tile([P, width], U32, name=name + "_codes", tag=tag or name + "_codes", align_bytes=64)
             scales = tile([P, width], U8, name + "_scales")
             nc.vector.quantize_mx(out=codes[:].bitcast(FP8X4), scales=scales[:], in_=src)
             return codes, scales
 
         offsets = sb.tile([P, S // 16], U16, name="offsets")
 
-        nc.sync.dma_start(offsets[:], offs)
         x_rows = xT.rearrange("(p j) t -> p j t", j=4)
         x_raw = []
         for j in range(4):
             x_raw.append(tile([P, T], F32, "x_raw%d" % j))
             nc.sync.dma_start(out=x_raw[j][:], in_=x_rows[:, j, :])
+            if j == 0:
+                nc.sync.dma_start(offsets[:], offs)
         w_raw = {}
         e_raw = {}
 
@@ -60,9 +63,10 @@ def tile_picked_edgeup_relu_e_kernel(tc, xT, eT, w1, w2, w3, w4_words, w4_scales
                 e_raw[q0 + q] = raw[:, :, q * Q:(q + 1) * Q]
 
         load_w(1, w1, 1)
-        load_w(2, w2, 1)
-        load_w(3, w3, 1)
-        load_e(0, 2)
+        load_w(2, w2, 2)
+        load_w(3, w3, 2)
+        load_e(0, 1)
+        load_e(1, 1)
         load_e(2, 1)
         load_e(3, 1)
 
@@ -88,7 +92,7 @@ def tile_picked_edgeup_relu_e_kernel(tc, xT, eT, w1, w2, w3, w4_words, w4_scales
         banks = [ps.tile([P, 4, Q], F32, name="h_acc%d" % q, tag="bank%d" % q) for q in range(NQ)]
 
         def weights(i, shares):
-            wb = sb.tile([P, 4, P, 4], BF16, name="w_bf%d" % i, tag="w_bf", align_bytes=64)
+            wb = sb.tile([P, 4, P, 4], BF16, name="w_bf%d" % i, tag="w_bf%d" % i, align_bytes=64)
             n = P // len(shares)
             for half, nv in enumerate(shares):
                 dst = wb[:, :, half * n:(half + 1) * n, :].rearrange("p t (b m) j -> p b j m t", m=2)
@@ -108,7 +112,10 @@ def tile_picked_edgeup_relu_e_kernel(tc, xT, eT, w1, w2, w3, w4_words, w4_scales
                     start=(start and t == 0), stop=(stop and t == 3))
 
         def edges_cast(q, nv):
-            eb = tile([P, Q, 4], BF16, "e_bf%d" % q)
+            if q == NQ - 1:
+                eb = late.tile([P, Q, 4], BF16, name="e_bf_last", offset=0, align_bytes=64)
+            else:
+                eb = tile([P, Q, 4], BF16, "e_bf%d" % q)
             dst = eb[:].rearrange("p (c i) j -> p c j i", i=4)
             src = e_raw[q].rearrange("p j (c i) -> p c j i", i=4)
             if nv > 0:
@@ -126,11 +133,11 @@ def tile_picked_edgeup_relu_e_kernel(tc, xT, eT, w1, w2, w3, w4_words, w4_scales
         for q in range(NQ):
             passes(q, w1q, xs, q * Q, True, False)
         eq = {}
-        w2q = weights(2, (60,))
+        w2q = weights(2, (0, 40))
         for q in range(NQ):
             passes(q, w2q, xd, q * Q, False, False)
-        w3q = weights(3, (84,))
-        ebs = {q: edges_cast(q, 32 * (q % 2)) for q in range(NQ)}
+        w3q = weights(3, (0, 52))
+        ebs = {q: edges_cast(q, 32 * (q // 2)) for q in range(NQ)}
         for q in range(NQ):
             eq[q] = edges_quant(q, ebs[q])
             passes(q, w3q, eq[q], 0, False, True)
@@ -144,20 +151,35 @@ def tile_picked_edgeup_relu_e_kernel(tc, xT, eT, w1, w2, w3, w4_words, w4_scales
                 rhs=hq[0][:].bitcast(FP8X4), rhs_scale=hq[1][:], start=True, stop=True)
 
         hqs = {}
-        for q in range(NQ):
-            hb = tile([P, Q, 4], BF16, "h_bf%d" % q)
+        ress = {}
+
+        def hidden(q):
             if q == 1:
+                hb = late.tile([P, Q, 4], BF16, name="h_bf_vector", offset=512, align_bytes=64)
                 nc.vector.tensor_scalar_max(out=hb[:], in0=banks[q][:].rearrange("p t v -> p v t"), scalar1=0.0)
             else:
+                hb = tile([P, Q, 4], BF16, "h_bf%d" % q)
                 nc.scalar.activation(out=hb[:], in_=banks[q][:].rearrange("p t v -> p v t"), func=ACT.Relu)
-            hqs[q] = quantize(hb[:].rearrange("p v t -> p (v t)"), Q, "h%d" % q)
-        for q in range(NQ - 1):
+            hqs[q] = quantize(hb[:].rearrange("p v t -> p (v t)"), Q, "h%d" % q,
+                              codes=late.tile([P, Q], U32, name="h0_codes", offset=0, align_bytes=64) if q == 0 else None)
+
+        def result(q):
             acc = ps.tile([P, 2, Q], F32, name="o_acc%d" % q, tag="bank%d" % (4 + q))
             for a in range(2):
                 second(a, hqs[q], acc[:, a, :])
             res = tile([P, 2, Q], F32, "res%d" % q)
-            nc.scalar.copy(out=res[:], in_=acc[:])
+            if q == NQ - 2:
+                nc.vector.tensor_copy(out=res[:], in_=acc[:])
+            else:
+                nc.scalar.copy(out=res[:], in_=acc[:])
+            ress[q] = res
             nc.sync.dma_start(out=out_rows[:, :, q * Q:(q + 1) * Q], in_=res[:])
+
+        for q in range(NQ - 1):
+            hidden(q)
+        hidden(NQ - 1)
+        for q in range(NQ - 1):
+            result(q)
         q = NQ - 1
         for a in range(2):
             acc = ps.tile([P, Q], F32, name="o_last%d" % a, tag="bank%d" % (7 if a == 0 else 0))

@@ -18,7 +18,7 @@ P = 128
 Q = 128
 NQ = V // Q
 NV = 640
-FIRST_V = 256
+FIRST_V = 128
 
 
 def tile_picked_edgeup_relu_e_kernel(tc, xT, eT, w1, w2, w3, w4_words, w4_scales, offs, out):
@@ -63,10 +63,9 @@ def tile_picked_edgeup_relu_e_kernel(tc, xT, eT, w1, w2, w3, w4_words, w4_scales
                 e_raw[q0 + q] = raw[:, :, q * Q:(q + 1) * Q]
 
         load_w(1, w1, 1)
-        load_w(2, w2, 2)
+        load_w(2, w2, 1)
         load_w(3, w3, 2)
-        load_e(0, 1)
-        load_e(1, 1)
+        load_e(0, 2)
         load_e(2, 1)
         load_e(3, 1)
 
@@ -133,7 +132,7 @@ def tile_picked_edgeup_relu_e_kernel(tc, xT, eT, w1, w2, w3, w4_words, w4_scales
         for q in range(NQ):
             passes(q, w1q, xs, q * Q, True, False)
         eq = {}
-        w2q = weights(2, (0, 40))
+        w2q = weights(2, (64,))
         for q in range(NQ):
             passes(q, w2q, xd, q * Q, False, False)
         w3q = weights(3, (0, 52))

@@ -64,7 +64,7 @@ def tile_picked_edgeup_relu_e_kernel(tc, xT, eT, w1, w2, w3, w4_words, w4_scales
 
         load_w(1, w1, 1)
         load_w(2, w2, 1)
-        load_w(3, w3, 2)
+        load_w(3, w3, 1)
         load_e(0, 2)
         load_e(2, 1)
         load_e(3, 1)
@@ -135,7 +135,7 @@ def tile_picked_edgeup_relu_e_kernel(tc, xT, eT, w1, w2, w3, w4_words, w4_scales
         w2q = weights(2, (64,))
         for q in range(NQ):
             passes(q, w2q, xd, q * Q, False, False)
-        w3q = weights(3, (0, 52))
+        w3q = weights(3, (84,))
         ebs = {q: edges_cast(q, 32 * (q // 2)) for q in range(NQ)}
         for q in range(NQ):
             eq[q] = edges_quant(q, ebs[q])

@@ -17,8 +17,12 @@ ACT = mybir.ActivationFunctionType
 P = 128
 Q = 128
 NQ = V // Q
-NV = 640
-FIRST_V = 128
+LAST = NQ - 1
+PER_COLUMN = 16
+VECTOR_PICKS = 576
+FIRST_PLANE_HELP = 256
+W_VECTOR_SHARE = (84, 56, 84)
+E_LOADS = ((0, 2), (2, 1), (3, 1))
 
 
 def tile_picked_edgeup_relu_e_kernel(tc, xT, eT, w1, w2, w3, w4_words, w4_scales, offs, out):
@@ -28,47 +32,33 @@ def tile_picked_edgeup_relu_e_kernel(tc, xT, eT, w1, w2, w3, w4_words, w4_scales
         late = ctx.enter_context(tc.tile_pool(name="late", bufs=1))
         ps = ctx.enter_context(tc.psum_pool(name="ps", bufs=1))
 
-        def tile(shape, dtype, name):
-            return sb.tile(shape, dtype, name=name, align_bytes=64)
+        def tile(shape, dtype, name, slot=None):
+            return sb.tile(shape, dtype, name=name, tag=slot or name, align_bytes=64)
 
-        def quantize(src, width, name, tag=None, codes=None):
+        def quantize(src, width, name, slot=None, codes=None):
             if codes is None:
-                codes = sb.tile([P, width], U32, name=name + "_codes", tag=tag or name + "_codes", align_bytes=64)
+                codes = tile([P, width], U32, name + "_codes", slot)
             scales = tile([P, width], U8, name + "_scales")
             nc.vector.quantize_mx(out=codes[:].bitcast(FP8X4), scales=scales[:], in_=src)
             return codes, scales
 
-        offsets = sb.tile([P, S // 16], U16, name="offsets")
-
-        x_rows = xT.rearrange("(p j) t -> p j t", j=4)
+        offsets = sb.tile([P, S // PER_COLUMN], U16, name="offsets")
+        x_planes = xT.rearrange("(p j) t -> p j t", j=4)
         x_raw = []
         for j in range(4):
             x_raw.append(tile([P, T], F32, "x_raw%d" % j))
-            nc.sync.dma_start(out=x_raw[j][:], in_=x_rows[:, j, :])
+            nc.sync.dma_start(out=x_raw[j][:], in_=x_planes[:, j, :])
             if j == 0:
                 nc.sync.dma_start(offsets[:], offs)
-        w_raw = {}
-        e_raw = {}
-
-        def load_w(i, w, parts):
-            n = H // parts
-            for part in range(parts):
-                w_raw[i, part] = tile([P, 4, n], F32, "w_raw%d%d" % (i, part))
-                nc.sync.dma_start(out=w_raw[i, part][:], in_=w.rearrange("(p j) c -> p j c", j=4)[:, :, part * n:(part + 1) * n])
-
-        def load_e(q0, nq):
+        w_raw = []
+        for i, w in enumerate((w1, w2, w3)):
+            w_raw.append(tile([P, 4, H], F32, "w_raw%d" % i))
+            nc.sync.dma_start(out=w_raw[i][:], in_=w.rearrange("(p j) c -> p j c", j=4))
+        e_raw = []
+        for q0, nq in E_LOADS:
             raw = tile([P, 4, nq * Q], F32, "e_raw%d" % q0)
             nc.sync.dma_start(out=raw[:], in_=eT.rearrange("(p j) v -> p j v", j=4)[:, :, q0 * Q:(q0 + nq) * Q])
-            for q in range(nq):
-                e_raw[q0 + q] = raw[:, :, q * Q:(q + 1) * Q]
-
-        load_w(1, w1, 1)
-        load_w(2, w2, 1)
-        load_w(3, w3, 1)
-        load_e(0, 2)
-        load_e(2, 1)
-        load_e(3, 1)
-
+            e_raw.extend(raw[:, :, q * Q:(q + 1) * Q] for q in range(nq))
         w4_codes = tile([P, N], U32, "w4_codes")
         w4_sc = tile([P, N], U8, "w4_sc")
         nc.vector.memset(w4_sc[:].bitcast(I32), 0)
@@ -76,33 +66,35 @@ def tile_picked_edgeup_relu_e_kernel(tc, xT, eT, w1, w2, w3, w4_words, w4_scales
         for g in range(4):
             nc.sync.dma_start(out=w4_sc[32 * g:32 * g + 4, :].bitcast(I32), in_=w4_scales[0, 4 * g:4 * g + 4, :].bitcast(I32))
 
+        def entries(first, end):
+            return offsets[:, first // PER_COLUMN:end // PER_COLUMN]
+
         picked = tile([P, S, 4], BF16, "picked")
         for u in range(2):
-            gathered = tile([P, 2, S - NV], BF16, "gathered%d" % u)
+            gathered = tile([P, 2, S - VECTOR_PICKS], BF16, "gathered%d" % u)
             for e in range(2):
                 j = 2 * u + e
-                nc.vector.tensor_copy(out=picked[:, :NV, j], in_=x_raw[j][:].indirect(offsets[:, :NV // 16]))
-                nv = FIRST_V if j == 0 else 0
-                if nv > 0:
-                    nc.vector.tensor_copy(out=gathered[:, e, :nv], in_=x_raw[j][:].indirect(offsets[:, NV // 16:(NV + nv) // 16]))
-                nc.scalar.activation(out=gathered[:, e, nv:], in_=x_raw[j][:].indirect(offsets[:, (NV + nv) // 16:]), func=ACT.Copy)
-            nc.scalar.copy(out=picked[:, NV:, 2 * u:2 * u + 2], in_=gathered[:].rearrange("p e v -> p v e"))
+                nc.vector.tensor_copy(out=picked[:, :VECTOR_PICKS, j], in_=x_raw[j][:].indirect(entries(0, VECTOR_PICKS)))
+                helped = FIRST_PLANE_HELP if j == 0 else 0
+                if helped > 0:
+                    nc.vector.tensor_copy(out=gathered[:, e, :helped],
+                                          in_=x_raw[j][:].indirect(entries(VECTOR_PICKS, VECTOR_PICKS + helped)))
+                nc.scalar.activation(out=gathered[:, e, helped:], in_=x_raw[j][:].indirect(entries(VECTOR_PICKS + helped, S)),
+                                     func=ACT.Copy)
+            nc.scalar.copy(out=picked[:, VECTOR_PICKS:, 2 * u:2 * u + 2], in_=gathered[:].rearrange("p e v -> p v e"))
 
         banks = [ps.tile([P, 4, Q], F32, name="h_acc%d" % q, tag="bank%d" % q) for q in range(NQ)]
 
-        def weights(i, shares):
-            wb = sb.tile([P, 4, P, 4], BF16, name="w_bf%d" % i, tag="w_bf%d" % i, align_bytes=64)
-            n = P // len(shares)
-            for half, nv in enumerate(shares):
-                dst = wb[:, :, half * n:(half + 1) * n, :].rearrange("p t (b m) j -> p b j m t", m=2)
-                src = w_raw[i, half][:].rearrange("p j (b m t) -> p b j m t", m=2, t=4)
-                if nv > 0:
-                    nc.vector.tensor_copy(out=dst[:, :nv // 2], in_=src[:, :nv // 2])
-                if nv < n:
-                    nc.scalar.copy(out=dst[:, nv // 2:], in_=src[:, nv // 2:])
-            return quantize(wb[:].rearrange("p t m j -> p (t m j)"), H, "w%d" % i)
+        def weight_codes(i):
+            rounded = tile([P, 4, P, 4], BF16, "w_bf%d" % i)
+            dst = rounded[:].rearrange("p t (b m) j -> p b j m t", m=2)
+            src = w_raw[i][:].rearrange("p j (b m t) -> p b j m t", m=2, t=4)
+            split = W_VECTOR_SHARE[i] // 2
+            nc.vector.tensor_copy(out=dst[:, :split], in_=src[:, :split])
+            nc.scalar.copy(out=dst[:, split:], in_=src[:, split:])
+            return quantize(rounded[:].rearrange("p t m j -> p (t m j)"), H, "w%d" % i)
 
-        def passes(q, wq, aq, col0, start, stop):
+        def first_passes(q, wq, aq, col0, start, stop):
             for t in range(4):
                 nc.tensor.matmul_mx(
                     out=banks[q][:, t, :],
@@ -110,83 +102,79 @@ def tile_picked_edgeup_relu_e_kernel(tc, xT, eT, w1, w2, w3, w4_words, w4_scales
                     rhs=aq[0][:, col0:col0 + Q].bitcast(FP8X4), rhs_scale=aq[1][:, col0:col0 + Q],
                     start=(start and t == 0), stop=(stop and t == 3))
 
-        def edges_cast(q, nv):
-            if q == NQ - 1:
-                eb = late.tile([P, Q, 4], BF16, name="e_bf_last", offset=0, align_bytes=64)
-            else:
-                eb = tile([P, Q, 4], BF16, "e_bf%d" % q)
-            dst = eb[:].rearrange("p (c i) j -> p c j i", i=4)
-            src = e_raw[q].rearrange("p j (c i) -> p c j i", i=4)
-            if nv > 0:
-                nc.vector.tensor_copy(out=dst[:, :nv], in_=src[:, :nv])
-            else:
-                nc.scalar.copy(out=dst, in_=src)
-            return eb
-
-        def edges_quant(q, eb):
-            return quantize(eb[:].rearrange("p v j -> p (v j)"), Q, "e%d" % q)
-
-        xs = quantize(picked[:, :V, :].rearrange("p v j -> p (v j)"), V, "x0")
-        w1q = weights(1, (72,))
-        xd = quantize(picked[:, V:, :].rearrange("p v j -> p (v j)"), V, "x1", tag="w_raw10")
+        src_q = quantize(picked[:, :V, :].rearrange("p v j -> p (v j)"), V, "src")
+        w1_q = weight_codes(0)
+        dst_q = quantize(picked[:, V:, :].rearrange("p v j -> p (v j)"), V, "dst", slot="w_raw0")
         for q in range(NQ):
-            passes(q, w1q, xs, q * Q, True, False)
-        eq = {}
-        w2q = weights(2, (64,))
+            first_passes(q, w1_q, src_q, q * Q, True, False)
+        w2_q = weight_codes(1)
         for q in range(NQ):
-            passes(q, w2q, xd, q * Q, False, False)
-        w3q = weights(3, (84,))
-        ebs = {q: edges_cast(q, 32 * (q // 2)) for q in range(NQ)}
-        for q in range(NQ):
-            eq[q] = edges_quant(q, ebs[q])
-            passes(q, w3q, eq[q], 0, False, True)
+            first_passes(q, w2_q, dst_q, q * Q, False, False)
+        w3_q = weight_codes(2)
 
         out_rows = out.rearrange("(a p) v -> p a v", p=P)
+        e_bf, e_q, h_q, ress = {}, {}, {}, {}
 
-        def second(a, hq, acc):
+        def round_edges(q):
+            if q == LAST:
+                e_bf[q] = late.tile([P, Q, 4], BF16, name="e_bf_last", offset=0, align_bytes=64)
+            else:
+                e_bf[q] = tile([P, Q, 4], BF16, "e_bf%d" % q)
+            dst = e_bf[q][:].rearrange("p (c i) j -> p c j i", i=4)
+            src = e_raw[q].rearrange("p j (c i) -> p c j i", i=4)
+            if q % 2 == 1:
+                nc.vector.tensor_copy(out=dst, in_=src)
+            else:
+                nc.scalar.copy(out=dst, in_=src)
+
+        def close_bank(q, slot=None):
+            e_q[q] = quantize(e_bf[q][:].rearrange("p v j -> p (v j)"), Q, "e%d" % q, slot)
+            first_passes(q, w3_q, e_q[q], 0, False, True)
+
+        def hidden(q):
+            src = banks[q][:].rearrange("p t v -> p v t")
+            if q == 2:
+                h_bf = late.tile([P, Q, 4], BF16, name="h_bf_vector", offset=512, align_bytes=64)
+                nc.vector.tensor_scalar_max(out=h_bf[:], in0=src, scalar1=0.0)
+            else:
+                h_bf = tile([P, Q, 4], BF16, "h_bf%d" % q)
+                nc.scalar.activation(out=h_bf[:], in_=src, func=ACT.Relu)
+            h_q[q] = quantize(h_bf[:].rearrange("p v t -> p (v t)"), Q, "h%d" % q,
+                              codes=late.tile([P, Q], U32, name="h0_codes", offset=0, align_bytes=64) if q == 0 else None)
+
+        def second_pass(q, a, acc):
             nc.tensor.matmul_mx(
                 out=acc,
                 lhsT=w4_codes[:, a * P:(a + 1) * P].bitcast(FP8X4), lhsT_scale=w4_sc[:, a * P:(a + 1) * P],
-                rhs=hq[0][:].bitcast(FP8X4), rhs_scale=hq[1][:], start=True, stop=True)
-
-        hqs = {}
-        ress = {}
-
-        def hidden(q):
-            if q == 1:
-                hb = late.tile([P, Q, 4], BF16, name="h_bf_vector", offset=512, align_bytes=64)
-                nc.vector.tensor_scalar_max(out=hb[:], in0=banks[q][:].rearrange("p t v -> p v t"), scalar1=0.0)
-            else:
-                hb = tile([P, Q, 4], BF16, "h_bf%d" % q)
-                nc.scalar.activation(out=hb[:], in_=banks[q][:].rearrange("p t v -> p v t"), func=ACT.Relu)
-            hqs[q] = quantize(hb[:].rearrange("p v t -> p (v t)"), Q, "h%d" % q,
-                              codes=late.tile([P, Q], U32, name="h0_codes", offset=0, align_bytes=64) if q == 0 else None)
+                rhs=h_q[q][0][:].bitcast(FP8X4), rhs_scale=h_q[q][1][:], start=True, stop=True)
 
         def result(q):
-            acc = ps.tile([P, 2, Q], F32, name="o_acc%d" % q, tag="bank%d" % (4 + q))
+            acc = ps.tile([P, 2, Q], F32, name="o_acc%d" % q, tag="bank%d" % (NQ + q))
             for a in range(2):
-                second(a, hqs[q], acc[:, a, :])
+                second_pass(q, a, acc[:, a, :])
             res = tile([P, 2, Q], F32, "res%d" % q)
-            if q == NQ - 2:
+            if q == LAST - 1:
                 nc.vector.tensor_copy(out=res[:], in_=acc[:])
             else:
                 nc.scalar.copy(out=res[:], in_=acc[:])
             ress[q] = res
             nc.sync.dma_start(out=out_rows[:, :, q * Q:(q + 1) * Q], in_=res[:])
 
-        for q in range(NQ - 1):
+        for q in range(NQ):
+            round_edges(q)
+        for q in range(NQ):
+            close_bank(q)
+        for q in range(NQ):
             hidden(q)
-        hidden(NQ - 1)
-        for q in range(NQ - 1):
+        for q in range(LAST):
             result(q)
-        q = NQ - 1
         for a in range(2):
-            acc = ps.tile([P, Q], F32, name="o_last%d" % a, tag="bank%d" % (7 if a == 0 else 0))
-            second(a, hqs[q], acc[:])
+            acc = ps.tile([P, Q], F32, name="o_last%d" % a, tag="bank%d" % (2 * NQ - 1 if a == 0 else 0))
+            second_pass(LAST, a, acc[:])
             res = tile([P, Q], F32, "res_last%d" % a)
             if a == 0:
                 nc.scalar.copy(out=res[:], in_=acc[:])
-                nc.scalar.dma_start(out=out_rows[:, a, q * Q:(q + 1) * Q], in_=res[:])
+                nc.scalar.dma_start(out=out_rows[:, a, LAST * Q:], in_=res[:])
             else:
                 nc.vector.tensor_copy(out=res[:], in_=acc[:])
-                nc.sync.dma_start(out=out_rows[:, a, q * Q:(q + 1) * Q], in_=res[:])
+                nc.sync.dma_start(out=out_rows[:, a, LAST * Q:], in_=res[:])

@@ -19,9 +19,9 @@ Q = 128
 NQ = V // Q
 LAST = NQ - 1
 PER_COLUMN = 16
-VECTOR_PICKS = 576
-FIRST_PLANE_HELP = 256
-W_VECTOR_SHARE = (84, 56, 84)
+VECTOR_PICKS = 640
+FIRST_PLANE_HELP = 128
+W_VECTOR_SHARE = (48, 60, 80)
 E_LOADS = ((0, 2), (2, 1), (3, 1))
 
 
@@ -103,8 +103,8 @@ def tile_picked_edgeup_relu_e_kernel(tc, xT, eT, w1, w2, w3, w4_words, w4_scales
                     start=(start and t == 0), stop=(stop and t == 3))
 
         src_q = quantize(picked[:, :V, :].rearrange("p v j -> p (v j)"), V, "src")
+        dst_q = quantize(picked[:, V:, :].rearrange("p v j -> p (v j)"), V, "dst")
         w1_q = weight_codes(0)
-        dst_q = quantize(picked[:, V:, :].rearrange("p v j -> p (v j)"), V, "dst", slot="w_raw0")
         for q in range(NQ):
             first_passes(q, w1_q, src_q, q * Q, True, False)
         w2_q = weight_codes(1)

@@ -22,6 +22,7 @@ PER_COLUMN = 16
 VECTOR_PICKS = 640
 FIRST_PLANE_HELP = 128
 W_VECTOR_SHARE = (48, 60, 80)
+E_VECTOR_SHARE = (0, Q, 48, Q)
 E_LOADS = ((0, 2), (2, 1), (3, 1))
 
 
@@ -116,16 +117,17 @@ def tile_picked_edgeup_relu_e_kernel(tc, xT, eT, w1, w2, w3, w4_words, w4_scales
         e_bf, e_q, h_q, ress = {}, {}, {}, {}
 
         def round_edges(q):
-            if q == LAST:
-                e_bf[q] = late.tile([P, Q, 4], BF16, name="e_bf_last", offset=0, align_bytes=64)
+            if q >= LAST - 1:
+                e_bf[q] = late.tile([P, Q, 4], BF16, name="e_bf_late%d" % q, offset=0, align_bytes=64)
             else:
                 e_bf[q] = tile([P, Q, 4], BF16, "e_bf%d" % q)
             dst = e_bf[q][:].rearrange("p (c i) j -> p c j i", i=4)
             src = e_raw[q].rearrange("p j (c i) -> p c j i", i=4)
-            if q % 2 == 1:
-                nc.vector.tensor_copy(out=dst, in_=src)
-            else:
-                nc.scalar.copy(out=dst, in_=src)
+            split = E_VECTOR_SHARE[q] // 4
+            if split > 0:
+                nc.vector.tensor_copy(out=dst[:, :split], in_=src[:, :split])
+            if split < Q // 4:
+                nc.scalar.copy(out=dst[:, split:], in_=src[:, split:])
 
         def close_bank(q, slot=None):
             e_q[q] = quantize(e_bf[q][:].rearrange("p v j -> p (v j)"), Q, "e%d" % q, slot)
@@ -160,10 +162,13 @@ def tile_picked_edgeup_relu_e_kernel(tc, xT, eT, w1, w2, w3, w4_words, w4_scales
             ress[q] = res
             nc.sync.dma_start(out=out_rows[:, :, q * Q:(q + 1) * Q], in_=res[:])
 
-        for q in range(NQ):
-            round_edges(q)
-        for q in range(NQ):
+        round_edges(0)
+        for q in range(LAST - 1):
+            round_edges(q + 1)
             close_bank(q)
+        close_bank(LAST - 1)
+        round_edges(LAST)
+        close_bank(LAST)
         for q in range(NQ):
             hidden(q)
         for q in range(LAST):
@@ -172,7 +177,7 @@ def tile_picked_edgeup_relu_e_kernel(tc, xT, eT, w1, w2, w3, w4_words, w4_scales
             acc = ps.tile([P, Q], F32, name="o_last%d" % a, tag="bank%d" % (2 * NQ - 1 if a == 0 else 0))
             second_pass(LAST, a, acc[:])
             res = tile([P, Q], F32, "res_last%d" % a)
-            if a == 0:
+            if a == 1:
                 nc.scalar.copy(out=res[:], in_=acc[:])
                 nc.scalar.dma_start(out=out_rows[:, a, LAST * Q:], in_=res[:])
             else:

@@ -21,8 +21,8 @@ LAST = NQ - 1
 PER_COLUMN = 16
 VECTOR_PICKS = 640
 FIRST_PLANE_HELP = 128
-W_VECTOR_SHARE = (48, 60, 80)
-E_VECTOR_SHARE = (0, Q, 48, Q)
+W_VECTOR_SHARE = (48, 60, 88)
+E_VECTOR_SHARE = (64, 64, 64, 128)
 E_LOADS = ((0, 2), (2, 1), (3, 1))
 
 
@@ -53,11 +53,14 @@ def tile_picked_edgeup_relu_e_kernel(tc, xT, eT, w1, w2, w3, w4_words, w4_scales
                 nc.sync.dma_start(offsets[:], offs)
         w_raw = []
         for i, w in enumerate((w1, w2, w3)):
-            w_raw.append(tile([P, 4, H], F32, "w_raw%d" % i))
+            if i == 2:
+                w_raw.append(late.tile([P, 4, H], F32, name="w_raw2", offset=0, align_bytes=64))
+            else:
+                w_raw.append(tile([P, 4, H], F32, "w_raw%d" % i))
             nc.sync.dma_start(out=w_raw[i][:], in_=w.rearrange("(p j) c -> p j c", j=4))
         e_raw = []
         for q0, nq in E_LOADS:
-            raw = tile([P, 4, nq * Q], F32, "e_raw%d" % q0)
+            raw = late.tile([P, 4, nq * Q], F32, name="e_raw%d" % q0, offset=16 * H + 16 * Q * q0, align_bytes=64)
             nc.sync.dma_start(out=raw[:], in_=eT.rearrange("(p j) v -> p j v", j=4)[:, :, q0 * Q:(q0 + nq) * Q])
             e_raw.extend(raw[:, :, q * Q:(q + 1) * Q] for q in range(nq))
         w4_codes = tile([P, N], U32, "w4_codes")
@@ -114,11 +117,11 @@ def tile_picked_edgeup_relu_e_kernel(tc, xT, eT, w1, w2, w3, w4_words, w4_scales
         w3_q = weight_codes(2)
 
         out_rows = out.rearrange("(a p) v -> p a v", p=P)
-        e_bf, e_q, h_q, ress = {}, {}, {}, {}
+        e_bf, e_q, h_q, ress, hb = {}, {}, {}, {}, {}
 
         def round_edges(q):
-            if q >= LAST - 1:
-                e_bf[q] = late.tile([P, Q, 4], BF16, name="e_bf_late%d" % q, offset=0, align_bytes=64)
+            if q == LAST:
+                e_bf[q] = late.tile([P, Q, 4], BF16, name="e_bf%d" % q, offset=16 * H + 32 * Q, align_bytes=64)
             else:
                 e_bf[q] = tile([P, Q, 4], BF16, "e_bf%d" % q)
             dst = e_bf[q][:].rearrange("p (c i) j -> p c j i", i=4)
@@ -133,16 +136,20 @@ def tile_picked_edgeup_relu_e_kernel(tc, xT, eT, w1, w2, w3, w4_words, w4_scales
             e_q[q] = quantize(e_bf[q][:].rearrange("p v j -> p (v j)"), Q, "e%d" % q, slot)
             first_passes(q, w3_q, e_q[q], 0, False, True)
 
-        def hidden(q):
+        def relu(q):
             src = banks[q][:].rearrange("p t v -> p v t")
-            if q == 2:
-                h_bf = late.tile([P, Q, 4], BF16, name="h_bf_vector", offset=512, align_bytes=64)
-                nc.vector.tensor_scalar_max(out=h_bf[:], in0=src, scalar1=0.0)
+            if q == 1:
+                h_bf = late.tile([P, Q, 4], BF16, name="h_bf1", offset=16 * H + 48 * Q, align_bytes=64)
             else:
                 h_bf = tile([P, Q, 4], BF16, "h_bf%d" % q)
+            if q == 1:
+                nc.vector.tensor_scalar_max(out=h_bf[:], in0=src, scalar1=0.0)
+            else:
                 nc.scalar.activation(out=h_bf[:], in_=src, func=ACT.Relu)
-            h_q[q] = quantize(h_bf[:].rearrange("p v t -> p (v t)"), Q, "h%d" % q,
-                              codes=late.tile([P, Q], U32, name="h0_codes", offset=0, align_bytes=64) if q == 0 else None)
+            hb[q] = h_bf
+
+        def hidden(q):
+            h_q[q] = quantize(hb[q][:].rearrange("p v t -> p (v t)"), Q, "h%d" % q)
 
         def second_pass(q, a, acc):
             nc.tensor.matmul_mx(
@@ -155,21 +162,22 @@ def tile_picked_edgeup_relu_e_kernel(tc, xT, eT, w1, w2, w3, w4_words, w4_scales
             for a in range(2):
                 second_pass(q, a, acc[:, a, :])
             res = tile([P, 2, Q], F32, "res%d" % q)
-            if q == LAST - 1:
-                nc.vector.tensor_copy(out=res[:], in_=acc[:])
-            else:
-                nc.scalar.copy(out=res[:], in_=acc[:])
+            nc.scalar.copy(out=res[:], in_=acc[:])
             ress[q] = res
             nc.sync.dma_start(out=out_rows[:, :, q * Q:(q + 1) * Q], in_=res[:])
 
         round_edges(0)
-        for q in range(LAST - 1):
-            round_edges(q + 1)
+        round_edges(1)
+        close_bank(0)
+        for q in range(1, NQ):
             close_bank(q)
-        close_bank(LAST - 1)
-        round_edges(LAST)
-        close_bank(LAST)
+            if q < LAST:
+                round_edges(q + 1)
+        relu(0)
+        relu(1)
         for q in range(NQ):
+            if q + 2 < NQ:
+                relu(q + 2)
             hidden(q)
         for q in range(LAST):
             result(q)

@@ -20,7 +20,6 @@ NQ = V // Q
 LAST = NQ - 1
 PER_COLUMN = 16
 VECTOR_PICKS = 640
-FIRST_PLANE_HELP = 128
 W_VECTOR_SHARE = (48, 60, 88)
 E_VECTOR_SHARE = (64, 64, 64, 128)
 E_LOADS = ((0, 2), (2, 1), (3, 1))
@@ -79,11 +78,7 @@ def tile_picked_edgeup_relu_e_kernel(tc, xT, eT, w1, w2, w3, w4_words, w4_scales
             for e in range(2):
                 j = 2 * u + e
                 nc.vector.tensor_copy(out=picked[:, :VECTOR_PICKS, j], in_=x_raw[j][:].indirect(entries(0, VECTOR_PICKS)))
-                helped = FIRST_PLANE_HELP if j == 0 else 0
-                if helped > 0:
-                    nc.vector.tensor_copy(out=gathered[:, e, :helped],
-                                          in_=x_raw[j][:].indirect(entries(VECTOR_PICKS, VECTOR_PICKS + helped)))
-                nc.scalar.activation(out=gathered[:, e, helped:], in_=x_raw[j][:].indirect(entries(VECTOR_PICKS + helped, S)),
+                nc.scalar.activation(out=gathered[:, e, :], in_=x_raw[j][:].indirect(entries(VECTOR_PICKS, S)),
                                      func=ACT.Copy)
             nc.scalar.copy(out=picked[:, VECTOR_PICKS:, 2 * u:2 * u + 2], in_=gathered[:].rearrange("p e v -> p v e"))
 

@@ -19,8 +19,9 @@ Q = 128
 NQ = V // Q
 LAST = NQ - 1
 PER_COLUMN = 16
-VECTOR_PICKS = 640
-W_VECTOR_SHARE = (48, 60, 88)
+VECTOR_PICKS = 576
+SCALAR_CUT = 800
+W_VECTOR_SHARE = (72, 60, 88)
 E_VECTOR_SHARE = (64, 64, 64, 128)
 E_LOADS = ((0, 2), (2, 1), (3, 1))
 
@@ -73,14 +74,15 @@ def tile_picked_edgeup_relu_e_kernel(tc, xT, eT, w1, w2, w3, w4_words, w4_scales
             return offsets[:, first // PER_COLUMN:end // PER_COLUMN]
 
         picked = tile([P, S, 4], BF16, "picked")
-        for u in range(2):
-            gathered = tile([P, 2, S - VECTOR_PICKS], BF16, "gathered%d" % u)
-            for e in range(2):
-                j = 2 * u + e
-                nc.vector.tensor_copy(out=picked[:, :VECTOR_PICKS, j], in_=x_raw[j][:].indirect(entries(0, VECTOR_PICKS)))
-                nc.scalar.activation(out=gathered[:, e, :], in_=x_raw[j][:].indirect(entries(VECTOR_PICKS, S)),
-                                     func=ACT.Copy)
-            nc.scalar.copy(out=picked[:, VECTOR_PICKS:, 2 * u:2 * u + 2], in_=gathered[:].rearrange("p e v -> p v e"))
+        runs = ((VECTOR_PICKS, SCALAR_CUT), (SCALAR_CUT, S))
+        gathered = [tile([P, 4, end - first], BF16, "gathered%d" % first) for first, end in runs]
+        for j in range(4):
+            nc.vector.tensor_copy(out=picked[:, :VECTOR_PICKS, j], in_=x_raw[j][:].indirect(entries(0, VECTOR_PICKS)))
+            for (first, end), planes in zip(runs, gathered):
+                nc.scalar.activation(out=planes[:, j, :], in_=x_raw[j][:].indirect(entries(first, end)), func=ACT.Copy)
+        for (first, end), planes in zip(runs, gathered):
+            nc.scalar.copy(out=picked[:, first:end, :].rearrange("p (c i) j -> p c j i", i=4),
+                           in_=planes[:].rearrange("p j (c i) -> p c j i", i=4))
 
         banks = [ps.tile([P, 4, Q], F32, name="h_acc%d" % q, tag="bank%d" % q) for q in range(NQ)]
 

@@ -22,7 +22,7 @@ PER_COLUMN = 16
 VECTOR_PICKS = 576
 SCALAR_CUT = 800
 W_VECTOR_SHARE = (72, 60, 88)
-E_VECTOR_SHARE = (64, 64, 64, 128)
+E_VECTOR_SHARE = (0, 88, 64, 128)
 E_LOADS = ((0, 2), (2, 1), (3, 1))
 
 

@@ -19,8 +19,7 @@ Q = 128
 NQ = V // Q
 LAST = NQ - 1
 PER_COLUMN = 16
-VECTOR_PICKS = 576
-SCALAR_CUT = 800
+VECTOR_PICKS = 512
 W_VECTOR_SHARE = (72, 60, 88)
 E_VECTOR_SHARE = (0, 88, 64, 128)
 E_LOADS = ((0, 2), (2, 1), (3, 1))
@@ -74,15 +73,9 @@ def tile_picked_edgeup_relu_e_kernel(tc, xT, eT, w1, w2, w3, w4_words, w4_scales
             return offsets[:, first // PER_COLUMN:end // PER_COLUMN]
 
         picked = tile([P, S, 4], BF16, "picked")
-        runs = ((VECTOR_PICKS, SCALAR_CUT), (SCALAR_CUT, S))
-        gathered = [tile([P, 4, end - first], BF16, "gathered%d" % first) for first, end in runs]
         for j in range(4):
             nc.vector.tensor_copy(out=picked[:, :VECTOR_PICKS, j], in_=x_raw[j][:].indirect(entries(0, VECTOR_PICKS)))
-            for (first, end), planes in zip(runs, gathered):
-                nc.scalar.activation(out=planes[:, j, :], in_=x_raw[j][:].indirect(entries(first, end)), func=ACT.Copy)
-        for (first, end), planes in zip(runs, gathered):
-            nc.scalar.copy(out=picked[:, first:end, :].rearrange("p (c i) j -> p c j i", i=4),
-                           in_=planes[:].rearrange("p j (c i) -> p c j i", i=4))
+            nc.scalar.activation(out=picked[:, VECTOR_PICKS:, j], in_=x_raw[j][:].indirect(entries(VECTOR_PICKS, S)), func=ACT.Copy)
 
         banks = [ps.tile([P, 4, Q], F32, name="h_acc%d" % q, tag="bank%d" % q) for q in range(NQ)]
 

@@ -42,6 +42,10 @@ def tile_picked_edgeup_relu_e_kernel(tc, xT, eT, w1, w2, w3, w4_words, w4_scales
             nc.vector.quantize_mx(out=codes[:].bitcast(FP8X4), scales=scales[:], in_=src)
             return codes, scales
 
+        warm = tile([P, 2, 8], F32, "warm")
+        nc.vector.memset(warm[:, 0, :], 0.0)
+        nc.scalar.activation(out=warm[:, 1, :], in_=warm[:, 0, :], func=ACT.Copy)
+
         offsets = sb.tile([P, S // PER_COLUMN], U16, name="offsets")
         x_planes = xT.rearrange("(p j) t -> p j t", j=4)
         x_raw = []

@@ -20,7 +20,7 @@ NQ = V // Q
 LAST = NQ - 1
 PER_COLUMN = 16
 VECTOR_PICKS = 512
-W_VECTOR_SHARE = (72, 60, 88)
+W_VECTOR_SHARE = (64, 80, 88)
 E_VECTOR_SHARE = (0, 88, 64, 128)
 E_LOADS = ((0, 2), (2, 1), (3, 1))
 

@@ -143,7 +143,7 @@ def tile_picked_edgeup_relu_e_kernel(tc, xT, eT, w1, w2, w3, w4_words, w4_scales
             hb[q] = h_bf
 
         def hidden(q):
-            h_q[q] = quantize(hb[q][:].rearrange("p v t -> p (v t)"), Q, "h%d" % q)
+            h_q[q] = quantize(hb[q][:].rearrange("p v t -> p (v t)"), Q, "h%d" % q, "h_slot%d" % (q % LAST))
 
         def second_pass(q, a, acc):
             nc.tensor.matmul_mx(
@@ -167,13 +167,21 @@ def tile_picked_edgeup_relu_e_kernel(tc, xT, eT, w1, w2, w3, w4_words, w4_scales
             close_bank(q)
             if q < LAST:
                 round_edges(q + 1)
-        relu(0)
-        relu(1)
         for q in range(NQ):
-            if q + 2 < NQ:
-                relu(q + 2)
-            hidden(q)
+            relu(q)
         for q in range(LAST):
+            hidden(q)
+        first = tile([P, 2, Q], F32, "res0")
+        for a in range(2):
+            acc = ps.tile([P, Q], F32, name="o_first%d" % a, tag="bank%d" % (NQ if a == 0 else 1))
+            second_pass(0, a, acc[:])
+            if a == 0:
+                nc.scalar.copy(out=first[:, a, :], in_=acc[:])
+            else:
+                nc.vector.tensor_copy(out=first[:, a, :], in_=acc[:])
+        nc.sync.dma_start(out=out_rows[:, :, :Q], in_=first[:])
+        hidden(LAST)
+        for q in range(1, LAST):
             result(q)
         for a in range(2):
             acc = ps.tile([P, Q], F32, name="o_last%d" % a, tag="bank%d" % (2 * NQ - 1 if a == 0 else 0))

from contextlib import ExitStack

import concourse.mybir as mybir

K, T, S, V, H, N = 512, 2048, 1024, 512, 512, 256
FLOPS = 2 * V * (3 * K * H + H * N)

F32 = mybir.dt.float32
BF16 = mybir.dt.bfloat16
I32 = mybir.dt.int32
U32 = mybir.dt.uint32
U16 = mybir.dt.uint16
U8 = mybir.dt.uint8
FP8X4 = mybir.dt.float8_e4m3fn_x4
ACT = mybir.ActivationFunctionType

P = 128
Q = 128
NQ = V // Q
LAST = NQ - 1
PER_COLUMN = 16
VECTOR_PICKS = 512
W_VECTOR_SHARE = (64, 80, 88)
E_VECTOR_SHARE = (0, 88, 64, 128)
E_LOADS = ((0, 2), (2, 1), (3, 1))


def tile_picked_edgeup_relu_e_kernel(tc, xT, eT, w1, w2, w3, w4_words, w4_scales, offs, out):
    nc = tc.nc
    with ExitStack() as ctx:
        sb = ctx.enter_context(tc.tile_pool(name="sb", bufs=1))
        late = ctx.enter_context(tc.tile_pool(name="late", bufs=1))
        ps = ctx.enter_context(tc.psum_pool(name="ps", bufs=1))

        def tile(shape, dtype, name, slot=None):
            return sb.tile(shape, dtype, name=name, tag=slot or name, align_bytes=64)

        def quantize(src, width, name, slot=None, codes=None):
            if codes is None:
                codes = tile([P, width], U32, name + "_codes", slot)
            scales = tile([P, width], U8, name + "_scales")
            nc.vector.quantize_mx(out=codes[:].bitcast(FP8X4), scales=scales[:], in_=src)
            return codes, scales

        warm = tile([P, 2, 8], F32, "warm")
        nc.vector.memset(warm[:, 0, :], 0.0)
        nc.scalar.activation(out=warm[:, 1, :], in_=warm[:, 0, :], func=ACT.Copy)

        offsets = sb.tile([P, S // PER_COLUMN], U16, name="offsets")
        x_planes = xT.rearrange("(p j) t -> p j t", j=4)
        x_raw = []
        for j in range(4):
            x_raw.append(tile([P, T], F32, "x_raw%d" % j))
            nc.sync.dma_start(out=x_raw[j][:], in_=x_planes[:, j, :])
            if j == 0:
                nc.sync.dma_start(offsets[:], offs)
        w_raw = []
        for i, w in enumerate((w1, w2, w3)):
            if i == 2:
                w_raw.append(late.tile([P, 4, H], F32, name="w_raw2", offset=0, align_bytes=64))
            else:
                w_raw.append(tile([P, 4, H], F32, "w_raw%d" % i))
            nc.sync.dma_start(out=w_raw[i][:], in_=w.rearrange("(p j) c -> p j c", j=4))
        e_raw = []
        for q0, nq in E_LOADS:
            raw = late.tile([P, 4, nq * Q], F32, name="e_raw%d" % q0, offset=16 * H + 16 * Q * q0, align_bytes=64)
            nc.sync.dma_start(out=raw[:], in_=eT.rearrange("(p j) v -> p j v", j=4)[:, :, q0 * Q:(q0 + nq) * Q])
            e_raw.extend(raw[:, :, q * Q:(q + 1) * Q] for q in range(nq))
        w4_codes = tile([P, N], U32, "w4_codes")
        w4_sc = tile([P, N], U8, "w4_sc")
        nc.vector.memset(w4_sc[:].bitcast(I32), 0)
        nc.sync.dma_start(out=w4_codes[:].bitcast(I32), in_=w4_words[0].rearrange("p n t -> p (n t)").bitcast(I32))
        for g in range(4):
            nc.sync.dma_start(out=w4_sc[32 * g:32 * g + 4, :].bitcast(I32), in_=w4_scales[0, 4 * g:4 * g + 4, :].bitcast(I32))

        def entries(first, end):
            return offsets[:, first // PER_COLUMN:end // PER_COLUMN]

        picked = tile([P, S, 4], BF16, "picked")
        for j in range(4):
            nc.vector.tensor_copy(out=picked[:, :VECTOR_PICKS, j], in_=x_raw[j][:].indirect(entries(0, VECTOR_PICKS)))
            nc.scalar.activation(out=picked[:, VECTOR_PICKS:, j], in_=x_raw[j][:].indirect(entries(VECTOR_PICKS, S)), func=ACT.Copy)

        banks = [ps.tile([P, 4, Q], F32, name="h_acc%d" % q, tag="bank%d" % q) for q in range(NQ)]

        def weight_codes(i):
            rounded = tile([P, 4, P, 4], BF16, "w_bf%d" % i)
            dst = rounded[:].rearrange("p t (b m) j -> p b j m t", m=2)
            src = w_raw[i][:].rearrange("p j (b m t) -> p b j m t", m=2, t=4)
            split = W_VECTOR_SHARE[i] // 2
            nc.vector.tensor_copy(out=dst[:, :split], in_=src[:, :split])
            nc.scalar.copy(out=dst[:, split:], in_=src[:, split:])
            return quantize(rounded[:].rearrange("p t m j -> p (t m j)"), H, "w%d" % i)

        def first_passes(q, wq, aq, col0, start, stop):
            for t in range(4):
                nc.tensor.matmul_mx(
                    out=banks[q][:, t, :],
                    lhsT=wq[0][:, t * P:(t + 1) * P].bitcast(FP8X4), lhsT_scale=wq[1][:, t * P:(t + 1) * P],
                    rhs=aq[0][:, col0:col0 + Q].bitcast(FP8X4), rhs_scale=aq[1][:, col0:col0 + Q],
                    start=(start and t == 0), stop=(stop and t == 3))

        src_q = quantize(picked[:, :V, :].rearrange("p v j -> p (v j)"), V, "src")
        dst_q = quantize(picked[:, V:, :].rearrange("p v j -> p (v j)"), V, "dst")
        w1_q = weight_codes(0)
        for q in range(NQ):
            first_passes(q, w1_q, src_q, q * Q, True, False)
        w2_q = weight_codes(1)
        for q in range(NQ):
            first_passes(q, w2_q, dst_q, q * Q, False, False)
        w3_q = weight_codes(2)

        out_rows = out.rearrange("(a p) v -> p a v", p=P)
        e_bf, e_q, h_q, ress, hb = {}, {}, {}, {}, {}

        def round_edges(q):
            if q == LAST:
                e_bf[q] = late.tile([P, Q, 4], BF16, name="e_bf%d" % q, offset=16 * H + 32 * Q, align_bytes=64)
            else:
                e_bf[q] = tile([P, Q, 4], BF16, "e_bf%d" % q)
            dst = e_bf[q][:].rearrange("p (c i) j -> p c j i", i=4)
            src = e_raw[q].rearrange("p j (c i) -> p c j i", i=4)
            split = E_VECTOR_SHARE[q] // 4
            if split > 0:
                nc.vector.tensor_copy(out=dst[:, :split], in_=src[:, :split])
            if split < Q // 4:
                nc.scalar.copy(out=dst[:, split:], in_=src[:, split:])

        def close_bank(q, slot=None):
            e_q[q] = quantize(e_bf[q][:].rearrange("p v j -> p (v j)"), Q, "e%d" % q, slot)
            first_passes(q, w3_q, e_q[q], 0, False, True)

        def relu(q):
            src = banks[q][:].rearrange("p t v -> p v t")
            if q == 1:
                h_bf = late.tile([P, Q, 4], BF16, name="h_bf1", offset=16 * H + 48 * Q, align_bytes=64)
            else:
                h_bf = tile([P, Q, 4], BF16, "h_bf%d" % q)
            if q == 1:
                nc.vector.tensor_scalar_max(out=h_bf[:], in0=src, scalar1=0.0)
            else:
                nc.scalar.activation(out=h_bf[:], in_=src, func=ACT.Relu)
            hb[q] = h_bf

        def hidden(q):
            h_q[q] = quantize(hb[q][:].rearrange("p v t -> p (v t)"), Q, "h%d" % q, "h_slot%d" % (q % LAST))

        def second_pass(q, a, acc):
            nc.tensor.matmul_mx(
                out=acc,
                lhsT=w4_codes[:, a * P:(a + 1) * P].bitcast(FP8X4), lhsT_scale=w4_sc[:, a * P:(a + 1) * P],
                rhs=h_q[q][0][:].bitcast(FP8X4), rhs_scale=h_q[q][1][:], start=True, stop=True)

        def result(q):
            acc = ps.tile([P, 2, Q], F32, name="o_acc%d" % q, tag="bank%d" % (NQ + q))
            for a in range(2):
                second_pass(q, a, acc[:, a, :])
            res = tile([P, 2, Q], F32, "res%d" % q)
            nc.scalar.copy(out=res[:], in_=acc[:])
            ress[q] = res
            nc.sync.dma_start(out=out_rows[:, :, q * Q:(q + 1) * Q], in_=res[:])

        round_edges(0)
        round_edges(1)
        close_bank(0)
        for q in range(1, NQ):
            close_bank(q)
            if q < LAST:
                round_edges(q + 1)
        for q in range(NQ):
            relu(q)
        for q in range(LAST):
            hidden(q)
        first = tile([P, 2, Q], F32, "res0")
        for a in range(2):
            acc = ps.tile([P, Q], F32, name="o_first%d" % a, tag="bank%d" % (NQ if a == 0 else 1))
            second_pass(0, a, acc[:])
            if a == 0:
                nc.scalar.copy(out=first[:, a, :], in_=acc[:])
            else:
                nc.vector.tensor_copy(out=first[:, a, :], in_=acc[:])
        nc.sync.dma_start(out=out_rows[:, :, :Q], in_=first[:])
        hidden(LAST)
        for q in range(1, LAST):
            result(q)
        for a in range(2):
            acc = ps.tile([P, Q], F32, name="o_last%d" % a, tag="bank%d" % (2 * NQ - 1 if a == 0 else 0))
            second_pass(LAST, a, acc[:])
            res = tile([P, Q], F32, "res_last%d" % a)
            if a == 1:
                nc.scalar.copy(out=res[:], in_=acc[:])
                nc.scalar.dma_start(out=out_rows[:, a, LAST * Q:], in_=res[:])
            else:
                nc.vector.tensor_copy(out=res[:], in_=acc[:])
                nc.sync.dma_start(out=out_rows[:, a, LAST * Q:], in_=res[:])
